import numpy as np, ml_dtypes
CORES = [9,25,41,57]
N = 4
BF = ml_dtypes.bfloat16
def f(rng, *shape):
    return (rng.standard_normal(shape, dtype=np.float32) * np.exp2(rng.integers(-2, 3, shape[:-1] + (1,)))).astype(BF)
def wide(rng, *shape):
    v = f(rng, *shape).astype(np.float32); k = shape[:-2] + (1, shape[-1])
    return (v * np.exp2(rng.integers(-6, 7, k)) * (rng.random(k) > 0.0625)).astype(BF)
def gentries(a):
    return np.ascontiguousarray(a.reshape(8, 16, -1).transpose(0, 2, 1)).reshape(8, -1)
def gtable(e):
    e = np.asarray(e); return np.ascontiguousarray(e.reshape(8, -1, 16).transpose(0, 2, 1)).reshape(128, -1).astype(np.int32)
B, M, W, S = 64, 64, 32, 2048
WL, WM, CB, CW = 3, 11, 12, 320
D, FR = 2048, 1
MB = M // 16
U, UB = CW // MB, S // MB
def book(rng, v):
    return (v.astype(np.float32) * (1 + rng.random(v.shape, dtype=np.float32))).astype(np.float32)
def parts(rng, k, s, exact):
    v = rng.integers(WL, WM + 1, k); t = s if exact else min(s, int(np.sum(v)))
    while np.sum(v) != t:
        e = 1 if np.sum(v) < t else -1
        i = np.flatnonzero(v < WM) if e > 0 else np.flatnonzero(v > WL)
        v[rng.permutation(i)[:abs(t - int(np.sum(v)))]] += e
    return v
def widths(rng):
    w = np.zeros((N, 8, B), np.int64)
    for q in range(N):
        for g in range(8):
            w[q, g] = parts(rng, B, UB, False); w[q, g, rng.integers(B)] = WL
    return w
def pick(rng, w, c, cand):
    left = U; lo = int(np.min(w[cand])); out = []
    for i in range(c):
        ok = cand[w[cand] <= left - (c - 1 - i) * lo]
        b = int(ok[rng.integers(len(ok))]); out.append(b); left -= int(w[b])
    return out
def wants(rng, w, uneven=False, full=None):
    L = np.zeros((N, 8, W), np.int64)
    for r in range(N):
        for g in range(8):
            q0 = -1
            own = np.repeat(rng.permutation(N), CB)
            if not uneven: own = rng.permutation(own)
            if full is not None:
                q0 = (r + 1 + g % (N - 1)) % N
                own = np.concatenate([np.full(CB, q0), own[own != q0]])
            c = np.bincount(own[:W], minlength=N); e = []
            for q in range(N):
                if q == q0:
                    e += [q * B + int(b) for b in full[q, g]]
                elif c[q]:
                    cand = np.arange(B)
                    if uneven and rng.random() < 0.5: cand = np.array([int(np.argmin(w[q, g])), int(rng.integers(B))])
                    e += [q * B + b for b in pick(rng, w[q, g], int(c[q]), cand)]
            L[r, g] = rng.permutation(np.array(e))
    return L
def make(rng, w, L, s):
    return {"strm": s.astype(np.int32), "wd": np.stack([gtable(u) for u in w]), "want": np.stack([gtable(u) for u in L]), "dic": book(rng, f(rng, N, 8 * FR, D))}
def setup_inputs(rng):
    w = widths(rng)
    return make(rng, w, wants(rng, w), rng.integers(0, 65536, (N, 8, S)))
def setup_inputs_full(rng):
    w = np.zeros((N, 8, B), np.int64); full = np.zeros((N, 8, CB), np.int64)
    for q in range(N):
        for g in range(8):
            p = np.concatenate([np.array([0, B - 1]), rng.permutation(np.arange(1, B - 1))])
            w[q, g, p[:CB]] = parts(rng, CB, U, True); w[q, g, p[CB:]] = parts(rng, B - CB, UB - U, True); full[q, g] = p[:CB]
    return make(rng, w, wants(rng, w, full=full), rng.integers(0, 65536, (N, 8, S)))
def setup_inputs_uneven(rng):
    w = widths(rng)
    return make(rng, w, wants(rng, w, uneven=True), rng.integers(0, 65536, (N, 8, S)))
def setup_inputs_ends(rng):
    w = np.full((N, 8, B), WL, np.int64); most = min(B - 1, (UB - B * WL) // (WM - WL))
    for q in range(N):
        for g in range(8):
            w[q, g, rng.permutation(B)[:rng.integers(0, most + 1)]] = WM
    s = rng.choice(np.array([0, 0, 1, 32768, 65535, 65535]), (N, 8, S))
    s = np.where(rng.random((N, 8, S)) < 0.25, rng.integers(0, 65536, (N, 8, S)), s)
    return make(rng, w, wants(rng, w), s)
def setup_inputs_spread(rng):
    d = setup_inputs(rng); d["dic"] = book(rng, wide(rng, N, 8 * FR, D)); return d
def check_inputs(d):
    try:
        bad = []
        if d["strm"].min() < 0 or d["strm"].max() > 65535: bad.append("words")
        if not np.isfinite(d["dic"].astype(np.float32)).all(): bad.append("finite")
        w = np.stack([gentries(u) for u in d["wd"]]).astype(np.int64); L = np.stack([gentries(u) for u in d["want"]]).astype(np.int64)
        if w.min() < WL or w.max() > WM: bad.append("widths")
        if (MB * np.sum(w, axis=2) > S).any(): bad.append("words of a column")
        if L.min() < 0 or L.max() >= N * B: return bad + ["wanted blocks"]
        n = np.zeros((N, 8, N), np.int64); m = np.zeros((N, 8, N), np.int64)
        for r in range(N):
            for g in range(8):
                q, b = L[r, g] // B, L[r, g] % B
                np.add.at(n[r, g], q, 1); np.add.at(m[r, g], q, MB * w[q, g, b])
        if n.max() > CB: bad.append("blocks of a pair")
        if m.max() > CW: bad.append("words of a pair")
        return bad
    except Exception:
        return ["shapes"]
def reference(strm, wd, want, dic):
    y = np.zeros((N, 8 * FR, W * M), dic.dtype)
    bit = (strm.astype(np.int64)[..., None] >> np.arange(16) & 1).reshape(N, 8, 16 * S)
    w = np.stack([gentries(wd[q]) for q in range(N)]).astype(np.int64)
    first = M * (np.add.accumulate(w, axis=2) - w)
    for r in range(N):
        L = gentries(want[r]).astype(np.int64)
        for g in range(8):
            q, b = L[g] // B, L[g] % B
            v = w[q, g, b][:, None]; at = first[q, g, b][:, None] + np.arange(M) * v
            code = np.zeros((W, M), np.int64)
            for k in range(WM):
                code += np.where(k < v, bit[q[:, None], g, np.minimum(at + k, 16 * S - 1)], 0) << k
            y[r, FR * g:FR * (g + 1)] = dic[r, FR * g:FR * (g + 1)][:, code.reshape(-1)]
    return {"y": y}

import math
from concourse.bass import DstId, RemoteDMATransfer
from concourse.mybir import AluOpType, ActivationFunctionType

A = AluOpType
AF = ActivationFunctionType
S = 2048
GFILL = 512

SCRATCH = {}
for _dt, _bufs in {
    "int32": dict(wnt=2, wdall=16, win=S, I0=2, I1=8, bi=2, P1=256, P2=256, P1m=256, di=8, dj=16, gi=128, ai=128),
    "float32": dict(dicw=S, yb=S, F1=8, C1=8, M=128, rmask=66, E=66, SS=66, K2r=12, K2=12, K2p=24, bf=2, c4=2,
                    tt=4, w4f=4, PF=4, EX=20, gb=8, pcs=256, Z=1728, m4r=32, mask4=32, res4=32, Wz=256, ra=32, rb=32,
                    rc=32, rd=32, Mw=128, mi=128),
    "bfloat16": dict(K1r=128, K1=128, Gt=128, gtm=128, ngt=128, ones=128, ident=128, Tq=256, qb=2, lh=256, rh=24,
                     w4=4, W5=4, PX=20, ne=144, R1=144, R2=144),
    "uint16": dict(wu=2, msg=12, lst=16, OL=32, wall=16, s4u=2, sel=16, cu=128),
    "float16": dict(snd=144, own=48, land=144),
}.items():
    for _k, _c in _bufs.items():
        SCRATCH[_k] = ("sbuf", [128, _c], _dt)
SCRATCH["AW"] = ("sbuf", [128, 9, 128], "bfloat16")
for _k in ("pc", "pq", "po", "pr0", "pr1", "pr2", "pr3", "pr4"):
    SCRATCH[_k] = ("psum", [128, 512], "float32")
NEV = 100
SEMAPHORES = ["aw", "ar1", "ar2", "ap1", "ap2", "ls"] + ["e%d" % i for i in range(NEV)]
LN2 = math.log(2.0)
MAGIC4 = 1.5 * 2.0 ** 25


def rank_program(g, core, T, topo):
    r = T.rank_of(core)
    if r is None:
        return
    cores = list(T.cores)
    n = len(cores)
    V, SC, PE, SY = g.vector, g.scalar, g.tensor, g.sync
    Q = {"g": g, "v": V, "s": SC, "t": PE, "y": SY}

    evs = []

    def ev():
        e = {"sem": T.sem["e%d" % len(evs)], "n": 0, "by": set()}
        evs.append(e)
        return e

    def tag(inst, e, k=1):
        assert not e["by"]
        inst.then_inc(e["sem"], k)
        e["n"] += k

    def wait(q, *es):
        for e in es:
            if q not in e["by"]:
                Q[q].wait_ge(e["sem"], e["n"])
                e["by"].add(q)

    def ts(e, out, in0, s1, op0, s2=None, op1=None):
        if op1 is None:
            tag(V.tensor_scalar(out, in0, s1, None, op0), e)
        else:
            tag(V.tensor_scalar(out, in0, s1, s2, op0, op1), e)

    def tt(e, out, a, b, op):
        tag(V.tensor_tensor(out, a, b, op), e)

    def cp(e, out, a):
        tag(V.tensor_copy(out, a), e)

    def iota(e, out, pat, base, cm, flt=True):
        if flt:
            tag(g.iota(out, pat, base, cm, allow_small_or_imprecise_dtypes=True), e)
        else:
            tag(g.iota(out, pat, base, cm), e)

    peer = [cores[(r + j) % n] for j in range(n)]
    back = [cores[(r - j) % n] for j in range(n)]
    eng = [e for e in topo.engines(core, peer[1]) if all(e in topo.engines(core, peer[j]) for j in (2, 3))]
    half = len(eng) // 2
    m_all = sum(1 << e for e in eng)
    m_lo = sum(1 << e for e in eng[:half])
    m_hi = sum(1 << e for e in eng[half:])

    def did(c):
        a = topo.addr(c)
        return DstId(rid=a[0], pnc=a[1])

    def col(t, j):
        return t[:, j:j + 1]

    def three(to, src, dstb, sem12, sem3, e12, e3_):
        wait("g", e12)
        g.remote_dma_fused([RemoteDMATransfer(dst_ids=[did(to[j])], dma_engine_mask=m, remote_sem=sem12,
                                              src=src(j), dst=dstb(j)) for j, m in ((1, m_lo), (2, m_hi))],
                           local_sem=T.sem.ls)
        wait("g", e3_)
        a = topo.addr(to[3])
        g.remote_dma(dstb(3), src(3), sem3, T.sem.ls, a[1], a[0], m_all)

    e_want, e_wd, e_win, e_strm = ev(), ev(), ev(), ev()
    tag(SY.dma_start(T.wnt[:], T.want[:]), e_want, 16)
    tag(SC.dma_start(T.wdall[:, 4 * r:4 * r + 4], T.wd[:]), e_wd, 16)
    tag(V.memset(T.win[:, 0:4], 0), e_win)
    tag(V.memset(T.win[:, S - 16:S], 0), e_win)
    wait("y", e_win)
    wait("s", e_win)
    for p in range(16):
        k0, s = (11 * p) >> 4, (11 * p) & 15
        sh = (k0 + 1 if s > 5 else k0) - 1
        q = SY if p % 2 == 0 else SC
        if sh < 0:
            tag(q.dma_start(T.win[p::16, 1:S], T.strm[:, 0:S - 1]), e_strm, 16)
        else:
            tag(q.dma_start(T.win[p::16, 0:S - sh], T.strm[:, sh:S]), e_strm, 16)

    e_p, e_M, e_k1, e_k2, e_gt = ev(), ev(), ev(), ev(), ev()
    iota(e_p, col(T.I1, 4), [[0, 1]], 0, 1, False)
    iota(e_p, col(T.I0, 0), [[0, 1]], 0, 11, False)
    iota(e_M, T.M[:], [[1, 128]], 0, 0)
    iota(e_k1, T.K1r[:], [[16, 8], [1, 4], [0, 4]], 0, 0)
    iota(e_k2, T.K2r[:], [[1024, 4], [4, 3]], 1024 * (129 + r), 0)
    iota(e_gt, T.Gt[:], [[16, 8], [0, 16]], 0, 0)

    e_c0, e_i, e_f, e_c11, e_c1, e1b, e2x = (ev() for _ in range(7))
    for q in range(4):
        tag(V.memset(T.Tq[:, 64 * q:64 * q + 64], float(129 + q)), e_c0)
    tag(V.memset(T.E[:], -2.5), e_c0)
    wait("v", e_p)
    pi = col(T.I1, 4)
    ts(e_i, col(T.I1, 0), pi, 15, A.bitwise_and)
    ts(e_i, col(T.I1, 1), pi, 112, A.bitwise_and)
    ts(e_i, col(T.I1, 2), pi, 3, A.bitwise_and)
    ts(e_i, col(T.I1, 3), col(T.I0, 0), 15, A.bitwise_and)
    wait("v", e_i)
    cp(e_f, T.F1[:, 0:5], T.I1[:, 0:5])
    pm, gbase, p3, sc, pf = (col(T.F1, j) for j in range(5))
    wait("v", e_f)
    ts(e_c11, col(T.C1, 3), pm, -11.0, A.mult, -21.0, A.add)
    ts(e_c11, col(T.C1, 4), pm, -11000.0, A.mult, -10000.0, A.add)
    ts(e_c1, col(T.C1, 0), p3, 64.0, A.mult)
    ts(e1b, col(T.C1, 1), sc, 5.0, A.is_gt, 16.0, A.mult)
    ts(e1b, col(T.C1, 2), sc, 5.0, A.is_le, -1000.0, A.mult)
    wait("v", e_M)
    ts(e_c1, T.rmask[:, 0:33], T.M[:, 0:33], pm, A.not_equal)
    ts(e_c1, T.rmask[:, 33:66], T.M[:, 0:33], -16.0, A.add, pm, A.not_equal)
    wait("v", e_k1)
    ts(e_c1, T.K1[:], T.K1r[:], gbase, A.subtract, -1.5, A.add)
    wait("v", e_k2)
    cut = 3 * (n - r)
    ts(e_c1, T.K2[:, 0:cut], T.K2r[:, 0:cut], 1.0 / 1024, A.mult)
    if cut < 12:
        ts(e_c1, T.K2[:, cut:12], T.K2r[:, cut:12], 1.0 / 1024, A.mult, -4.0, A.add)

    e_e, e_r = ev(), ev()
    wait("s", e_M, e_c11)
    for w in range(3, 12):
        tag(SC.activation(T.ne[:, 16 * w - 48:16 * w - 32], T.M[:, 1:17], AF.Identity, bias=col(T.C1, 3), scale=float(w)), e_e)
    for w in range(3, 12):
        tag(SC.activation(T.R1[:, 16 * w - 48:16 * w - 32], T.M[:, 0:16], AF.Relu, bias=col(T.C1, 4), scale=1000.0 * w), e_r)
    wait("s", e_e)
    tag(SC.activation(T.R2[:], T.ne[:], AF.Relu, bias=-20000.0, scale=-1000.0), e_r)

    wait("g", e_wd)
    mine = T.wdall[:, 4 * r:4 * r + 4]
    a1 = topo.addr(peer[1])
    g.remote_dma(mine, mine, T.sem.aw, T.sem.ls, a1[1], a1[0], m_all)
    nls = len(eng)

    e1, e2, e2b, e2c, e3, e3b, e4, e4b, e5a, e5b, e_id = (ev() for _ in range(11))
    wait("v", e_want)
    cp(e1, T.wu[:], T.wnt[:])
    ts(e1, T.qb[:], T.wnt[:], 1.0 / 64, A.mult, 128.5078125, A.add)
    ts(e2c, T.bi[:], T.wnt[:], 63, A.bitwise_and)
    wait("v", e1b)
    ts(e2x, col(T.EX, 16), col(T.C1, 1), sc, A.subtract)
    wait("v", e1, e_c0, e_c1)
    for h in range(2):
        ts(e2, T.E[:, 33 * h:33 * h + 32], T.Tq[:, 0:256].indirect(T.wu[:, 0:2]), col(T.qb, h), A.is_equal)
    for h in range(2):
        ts(e2b, T.K2p[:, 12 * h:12 * h + 12], T.K2[:], col(T.qb, h), A.subtract, 1024.0, A.mult)
    wait("v", e2)
    tag(V.tensor_tensor_scan(T.SS[:], T.rmask[:], T.E[:], 0.0, A.mult, A.add), e3)
    wait("v", e2c)
    cp(e2b, T.bf[:], T.bi[:])
    ts(e2x, col(T.EX, 17), col(T.C1, 2), sc, A.subtract)
    wait("v", e3)
    ts(e4, T.c4[:], T.SS[:, 32:66:33], MAGIC4, A.add, -MAGIC4, A.add)
    ts(e2x, T.EX[:, 18:20], T.F1[:, 3:5], -1.0, A.mult, -1.0, A.add)
    ts(e2x, T.EX[:, 0:16], T.M[:, 0:16], -18.0, A.add)
    wait("v", e4, e2b)
    for h, e in ((0, e5a), (1, e5b)):
        ts(e, T.lh[:, 128 * h:128 * h + 128], T.K1[:], col(T.c4, h), A.add, col(T.SS, 32 + 33 * h), A.is_equal)
        ts(e, T.rh[:, 12 * h:12 * h + 12], T.K2p[:, 12 * h:12 * h + 12], col(T.c4, h), A.is_equal, col(T.bf, h), A.mult)
    e_pq, e_pc, e6 = ev(), ev(), ev()
    wait("t", e5a)
    PE.matmul(T.pq[:, 0:12], T.lh[:, 0:128], T.rh[:, 0:12], True, False)
    wait("t", e5b)
    tag(PE.matmul(T.pq[:, 0:12], T.lh[:, 128:256], T.rh[:, 12:24], False, True), e_pq)
    wait("v", e_wd, e_gt)
    ts(e3b, T.w4[:], mine, 4.0, A.mult)
    ts(e3b, T.ngt[:], T.Gt[:], pf, A.is_gt, -1.0, A.mult)
    wait("v", e_pq)
    ts(e6, T.msg[:], T.pq[:, 0:12], col(T.C1, 0), A.add)

    three(peer, lambda j: T.msg[:, 3 * j:3 * j + 3], lambda j: T.lst[:, 3 * j - 3:3 * j], T.sem.ar1, T.sem.ar2, e6, e6)
    g.remote_dma_fused([RemoteDMATransfer(dst_ids=[did(peer[2]), did(peer[3])], dma_engine_mask=m_all,
                                          remote_sem=T.sem.aw, srcs=[mine], dsts=[mine, mine])], local_sem=T.sem.ls)
    nls += 3 * len(eng)
    e_m4, e_fill = ev(), ev()
    iota(e_m4, T.m4r[:], [[0, 8], [4, 4]], 0, 0)
    iota(e_fill, T.dicw[:, 0:GFILL], [[0, GFILL]], 0, 0)

    e_px, e_o, e_o1, e_eb, e_aw, e_gb = (ev() for _ in range(6))
    wait("s", e2x)
    tag(SC.activation(T.PX[:], T.EX[:], AF.Exp, scale=LN2), e_px)
    ts(e3b, T.gtm[:], T.M[:], pf, A.is_gt)
    ts(e4b, T.ones[:], T.Gt[:], gbase, A.is_equal)
    ts(e4b, T.tt[:], T.M[:, 0:4], 0.25, A.mult)
    ts(e4b, T.w4f[:], mine, 4.0, A.mult)
    wait("v", e3b)
    tag(V.tensor_tensor_scan(T.W5[:, 1:4], T.w4[:, 0:3], T.w4[:, 0:3], 0.0, A.add, A.max), e4b)
    ts(e_id, T.ident[:], T.M[:], pf, A.is_equal)
    ts(e_gb, T.gb[:], T.Gt[:, 0:128:16], gbase, A.not_equal, -1000.0, A.mult)
    wait("t", e3b)
    PE.matmul(T.pc[:, 0:4], T.gtm[:], T.w4[:], True, False)
    PE.matmul(T.pc[:, 0:4], T.ngt[:], T.w4[:], False, False)
    wait("t", e4b)
    tag(PE.matmul(T.pc[:, 1:4], T.ones[:], T.W5[:, 1:4], False, True), e_pc)
    wait("t", e_id, e_e, e_r)
    PE.matmul(T.po[:, 0:144], T.ident[:], T.ne[:], True, False)
    PE.matmul(T.po[:, 0:144], T.ident[:], T.R1[:], False, False)
    tag(PE.matmul(T.po[:, 0:144], T.ident[:], T.R2[:], False, True), e_eb)
    wait("v", e4b, e_pc)
    for bh in range(4):
        ts(e_o, T.OL[:, 16 + bh:32:4], T.tt[:], col(T.w4f, bh), A.mult, col(T.pc, bh), A.add)
    wait("v", e_px)
    ts(e_o1, col(T.C1, 5), col(T.PX, 18), -0.5, A.add)
    cp(e_o1, T.PF[:, 0:2], T.PX[:, 16:18])
    wait("v", e_o)
    ts(e_o1, T.OL[:, 0:16], T.OL[:, 16:32], 1.0, A.add)
    wait("s", e_eb, e_gb)
    for gg in range(8):
        tag(SC.activation(T.AW[:, :, 16 * gg:16 * gg + 16], T.po[:, 0:144], AF.Exp, bias=col(T.gb, gg), scale=-LN2), e_aw)
    wait("s", e_aw)
    for a in range(GFILL, S, 768):
        tag(SC.activation(T.dicw[:, a:a + 768], T.AW[:, 0:6, :], AF.Copy), e_fill)
    e_dic = ev()
    wait("y", e_fill)
    tag(SY.dma_start(T.dicw[0::16, :], T.dic[:]), e_dic, 16)

    e_p1, e_p2, e_p1m, e_pcs = ev(), ev(), ev(), ev()
    wait("v", e_o1, e_strm)
    ts(e_p1, T.P1[:], T.win[:, 0:S].indirect(T.OL[:, 0:16]), col(T.PF, 0), A.mult, col(T.C1, 5), A.add)
    ts(e_p2, T.P2[:], T.win[:, 0:S].indirect(T.OL[:, 16:32]), col(T.PF, 1), A.mult, col(T.C1, 5), A.add)
    wait("v", e_p1)
    ts(e_p1m, T.P1m[:], T.P1[:], 2047, A.bitwise_and)
    wait("v", e_p1m, e_p2)
    tt(e_pcs, T.pcs[:], T.P1m[:], T.P2[:], A.add)
    wait("v", e_pcs)

    e_s12, e_s3, e_own = ev(), ev(), ev()
    V.wait_ge(T.sem.ar1, 2 * half)
    cp(e_s12, T.snd[:, 0:96], T.pcs[:, 0:256].indirect(T.lst[:, 0:6]))
    V.wait_ge(T.sem.ar2, len(eng))
    cp(e_s3, T.snd[:, 96:144], T.pcs[:, 0:256].indirect(T.lst[:, 6:9]))
    wait("v", e6)
    cp(e_own, T.own[:], T.pcs[:, 0:256].indirect(T.msg[:, 0:3]))
    three(back, lambda j: T.snd[:, 48 * j - 48:48 * j], lambda j: T.land[:, 48 * j - 48:48 * j], T.sem.ap1, T.sem.ap2,
          e_s12, e_s3)
    nls += 2 * len(eng)

    e_po, e_z = ev(), ev()
    wait("t", e_aw, e_own)
    for w in range(9):
        tag(PE.matmul(T.po[:, 48 * w:48 * w + 48], T.AW[:, w, :], T.own[:], True, True), e_po)
    wait("s", e_po)
    tag(SC.activation(T.Z[:, 0:432], T.po[:, 0:432], AF.Copy), e_z)

    f1, f2, f3, f4, f5, f6, f7, f8, f9 = (ev() for _ in range(9))
    tt(f1, col(T.C1, 6), pm, p3, A.subtract)
    ts(f1, T.s4u[:], T.SS[:, 32:66:33], 4.0, A.mult, 6.0, A.add)
    V.wait_ge(T.sem.aw, 3 * len(eng))
    cp(f1, T.wall[:], T.wdall[:])
    wait("v", e_m4)
    ts(f2, T.res4[:], T.m4r[:], 0.0, A.not_equal)
    wait("v", f1)
    ts(f2, T.mask4[:], T.m4r[:], col(T.C1, 6), A.is_equal)
    cp(f2, T.ra[:], T.M[:, 0:64].indirect(T.s4u[:, 0:2]))
    for q in range(4):
        j = (q - r) % n
        mul = 2048 + (48, 96, 96, 48)[j]
        add = (0, 432, 480, 1296)[j] - 3 * mul
        ts(f2, T.Wz[:, 64 * q:64 * q + 64], T.M[:, 0:16].indirect(T.wall[:, 4 * q:4 * q + 4]),
           float(mul), A.mult, float(add), A.add)
    wait("v", f2)
    tt(f3, T.rb[:], T.Wz[:, 0:256].indirect(T.wu[:, 0:2]), T.ra[:], A.add)
    wait("v", f3)
    tt(f4, T.rc[:], T.rb[:], T.mask4[:], A.mult)
    wait("v", f4)
    tag(V.tensor_tensor_scan(T.rd[:], T.res4[:], T.rc[:], 0.0, A.mult, A.add), f5)
    wait("v", f5)
    ts(f6, T.di[:], T.rd[:, 3:32:4], p3, A.add)
    wait("v", f6)
    ts(f7, T.dj[:, 0:8], T.di[:], 2047, A.bitwise_and)
    ts(f7, T.dj[:, 8:16], T.di[:], 11, A.arith_shift_right)
    wait("v", f7)
    cp(f8, T.sel[:], T.dj[:])
    wait("v", f8)
    cp(f9, T.Mw[:], T.PX[:, 0:16].indirect(T.sel[:, 8:16]))

    jobs = []
    PE.wait_ge(T.sem.ap1, 2 * half)
    for i, b in enumerate((T.pr0, T.pr1, T.pr2)):
        e = ev()
        for u in range(3):
            tag(PE.matmul(b[:, 96 * u:96 * u + 96], T.AW[:, 3 * i + u, :], T.land[:, 0:96], True, True), e)
        jobs.append((e, T.Z[:, 432 + 288 * i:720 + 288 * i], b[:, 0:288]))
    PE.wait_ge(T.sem.ap2, len(eng))
    wait("t", e6)
    for i, b in enumerate((T.pr3, T.pr4, T.pq)):
        e = ev()
        for u in range(3):
            tag(PE.matmul(b[:, 48 * u:48 * u + 48], T.AW[:, 3 * i + u, :], T.land[:, 96:144], True, True), e)
        jobs.append((e, T.Z[:, 1296 + 144 * i:1440 + 144 * i], b[:, 0:144]))
    for i, (e, out, src) in enumerate(jobs):
        if i % 2 == 1:
            wait("v", e)
            cp(e_z, out, src)
        else:
            wait("s", e)
            tag(SC.activation(out, src, AF.Copy), e_z)

    hs = [slice(0, 64), slice(64, 128)]
    eg, ea_, em, ec = ([ev(), ev()] for _ in range(4))
    wait("v", e_z, f9)
    for h in range(2):
        cp(eg[h], T.gi[:, hs[h]], T.Z[:, 0:1728].indirect(T.sel[:, 4 * h:4 * h + 4]))
    for h in range(2):
        wait("v", eg[h])
        ts(ea_[h], T.ai[:, hs[h]], T.gi[:, hs[h]], (1 << 21) - 1, A.bitwise_and)
    for h in range(2):
        wait("v", ea_[h])
        tt(em[h], T.mi[:, hs[h]], T.ai[:, hs[h]], T.Mw[:, hs[h]], A.mult)
    for h in range(2):
        wait("v", em[h])
        ts(ec[h], T.cu[:, hs[h]], T.mi[:, hs[h]], -0.5 + 2.0 ** -11, A.add)
    e_y0, e_y1, e_out = ev(), ev(), ev()
    wait("s", e_dic, ec[0])
    tag(SC.activation(T.yb[:, 0:1024], T.dicw[:, 0:S].indirect(T.cu[:, 0:64]), AF.Copy), e_y0)
    wait("v", e_dic, ec[1])
    cp(e_y1, T.yb[:, 1024:2048], T.dicw[:, 0:S].indirect(T.cu[:, 64:128]))
    wait("s", e_y0)
    tag(SC.dma_start(T.y[:, 0:1024], T.yb[0::16, 0:1024]), e_out, 16)
    wait("y", e_y1)
    tag(SY.dma_start(T.y[:, 1024:2048], T.yb[0::16, 1024:2048]), e_out, 16)
    wait("y", e_out)
    g.wait_ge(T.sem.ls, nls)
    for e in evs:
        if e["n"] and not e["by"]:
            wait("g", e)
